import numpy as np
import ml_dtypes


def mxq(x, axis, fmt="e4m3"):
    dtype, down = {"e4m3": (ml_dtypes.float8_e4m3fn, 7), "e5m2": (ml_dtypes.float8_e5m2, 14)}[fmt]
    v = np.moveaxis(np.asarray(x, np.float32).astype(ml_dtypes.bfloat16).astype(np.float64), axis, -1)
    blocks = v.reshape(v.shape[:-1] + (-1, 32))
    amax = np.abs(blocks).max(-1, keepdims=True)
    byte = np.maximum(np.where(amax > 0, np.frexp(amax)[1] - 1 + 127, 0) - down, 1)
    scale = np.exp2(byte - 127.0)
    codes = (blocks / scale).astype(np.float32).astype(dtype).astype(np.float64)
    return np.moveaxis((codes * scale).reshape(v.shape), -1, axis)


WIDE = False


def mx_kscale(k):
    if not WIDE:
        return np.ones(k)
    levels = np.array([10, -10, 5, -5, 0])
    if k % 512:
        return np.exp2(np.random.permutation(np.resize(levels, k // 32))).repeat(32)
    a = np.empty((k // 512, 16))
    for p in range(k // 512):
        a[p, :8] = np.random.permutation(np.resize(levels, 8))
        for g in range(8):
            far = levels[np.abs(levels - a[p, g]) >= 10]
            a[p, g + 8] = far[np.random.randint(len(far))]
    return np.exp2(a.ravel()).repeat(32)


def f64(x):
    return np.asarray(x).astype(np.float64)


def striped8(idx):
    return np.asarray(idx).reshape(8, -1, 16).transpose(0, 2, 1).reshape(128, -1).astype(np.uint16)


def unstriped8(offs):
    return offs.reshape(8, 16, -1).transpose(0, 2, 1).reshape(8, -1).astype(np.int64)


def pick8(x, idx, run):
    r = np.arange(len(x))
    return x[r[:, None], idx[r % (8 * run) // run]]


E2M1 = np.array([0.0, 0.5, 1.0, 1.5, 2.0, 3.0, 4.0, 6.0, -0.0, -0.5, -1.0, -1.5, -2.0, -3.0, -4.0, -6.0])


def pack_weight(w, fmt):
    k, n = w.shape
    w = f64(np.asarray(w, np.float32).astype(ml_dtypes.bfloat16)).reshape(k // 32, 32, n)
    amax = np.abs(w).max(1)
    if fmt == "e4m3":
        byte = np.frexp(amax)[1] - 1 + 127 - 7
    else:
        mant, ex = np.frexp(amax / 6.0)
        byte = np.where(mant > 0.5, ex, ex - 1) + 127
    byte = np.clip(np.where(amax > 0, byte, 1), 1, 254)
    scaled = (w * np.exp2(127.0 - byte)[:, None, :]).reshape(k, n).astype(np.float32)
    by_word = np.ascontiguousarray(scaled.reshape(k // 512, 128, 4, n).transpose(0, 1, 3, 2))
    if fmt == "e4m3":
        words = by_word.astype(ml_dtypes.float8_e4m3fn).view(np.uint8)
    else:
        c = by_word.astype(ml_dtypes.float4_e2m1fn).view(np.uint8) & 0xF
        words = (c[..., 0::2] | (c[..., 1::2] << 4)).reshape(k // 512, 128, 2 * n)
    return np.ascontiguousarray(words), np.ascontiguousarray(byte.astype(np.uint8).reshape(k // 512, 16, n))


def unpack_weight(words, scales, fmt):
    g, _, n = scales.shape
    words = np.ascontiguousarray(words).reshape(g, 128, n, -1)
    if fmt == "e4m3":
        vals = words.view(ml_dtypes.float8_e4m3fn).astype(np.float64)
    else:
        nib = np.empty((g, 128, n, 4), np.uint8)
        nib[..., 0::2] = words & 0xF
        nib[..., 1::2] = words >> 4
        vals = E2M1[nib]
    vals = vals * np.repeat(np.exp2(scales.astype(np.float64) - 127.0), 8, axis=1)[..., None]
    return vals.transpose(0, 1, 3, 2).reshape(g * 512, n)


D, T, Q, I, E = 512, 1024, 128, 512, 512


def setup_inputs():
    n = np.random.standard_normal
    idx = np.stack([np.random.permutation(T)[:I] for _ in range(8)])
    idx2 = np.stack([np.random.permutation(T)[:I] for _ in range(8)])
    fd = mx_kscale(D)
    ft = mx_kscale(T)
    keysp = pack_weight(n((D, T)) / fd[:, None], "e4m3")
    return {
        "query": (n((D, Q)) * 0.6 / np.sqrt(D) * fd[:, None]).astype(np.float32),
        "keys_words": keysp[0],
        "keys_scales": keysp[1],
        "share": (np.random.uniform(0.2, 0.9, (1, I))).astype(np.float32),
        "fac": (np.random.uniform(8.0, 32.0, (1, T)) * ft).astype(np.float32),
        "vals": (n((T, E)) / ft[:, None]).astype(np.float32),
        "offs": striped8(idx),
        "offs2": striped8(idx2),
    }


def reference(query, keys_words, keys_scales, share, fac, vals, offs, offs2):
    idx = unstriped8(offs)
    idx2 = unstriped8(offs2)
    keysu = unpack_weight(keys_words, keys_scales, "e4m3")
    queryq = mxq(f64(query), 0, "e4m3")
    a = queryq.T @ keysu
    m1 = np.max(a, axis=1, keepdims=True)
    p = np.exp(a - m1)
    r = np.exp(pick8(a, idx, 16) - m1)
    ra = r * f64(share)
    rf = np.zeros((Q, T))
    rf[np.arange(Q)[:, None], idx[np.arange(Q) % 128 // 16]] = r
    rg = np.zeros((Q, T))
    rg[np.arange(Q)[:, None], idx2[np.arange(Q) % 128 // 16]] = ra
    w = (p - rf + rg) * f64(fac) / np.sum(p, axis=1, keepdims=True)
    wt = w.T
    wtq = mxq(wt, 0, "e4m3")
    valsq = mxq(f64(vals), 0, "e4m3")
    o = wtq.T @ valsq
    return o

@@ -1,0 +1,230 @@
+from contextlib import ExitStack
+
+import concourse.mybir as mybir
+from concourse.masks import make_identity
+
+D, T, Q, I, E = 512, 1024, 128, 512, 512
+FLOPS = 2 * Q * D * T + 2 * Q * T * E
+
+F32 = mybir.dt.float32
+BF16 = mybir.dt.bfloat16
+I32 = mybir.dt.int32
+U32 = mybir.dt.uint32
+U16 = mybir.dt.uint16
+U8 = mybir.dt.uint8
+FP8X4 = mybir.dt.float8_e4m3fn_x4
+ALU = mybir.AluOpType
+ACT = mybir.ActivationFunctionType
+
+P = 128
+PACK = 4
+K_PASS = P * PACK
+PASSES = T // K_PASS
+BANK = 512
+E_HALF = E // 2
+I_HALF = I // 2
+LINE = 4
+P_FIRST = 384
+E_EARLY = 128
+
+
+def interleave_views(dst, src):
+    return (
+        dst.rearrange("p (c i) j -> p c j i", i=LINE),
+        src.rearrange("p j (c i) -> p c j i", i=LINE),
+    )
+
+
+def tile_attend_passedon_heads_kernel(tc, query, keys_words, keys_scales, share, fac, vals, offs, offs2, out):
+    nc = tc.nc
+    with ExitStack() as ctx:
+        keep = ctx.enter_context(tc.tile_pool(name="keep", bufs=1))
+        psum = ctx.enter_context(tc.psum_pool(name="psum", bufs=1))
+
+        k_scales = keep.tile([P, T], U8, name="k_scales", align_bytes=64)
+        nc.vector.memset(k_scales[:].bitcast(I32), 0)
+        q_raw = keep.tile([P, PACK, Q], F32, name="q_raw")
+        nc.sync.dma_start(out=q_raw[:], in_=query.rearrange("(p j) q -> p j q", j=PACK))
+        for quad in range(4):
+            nc.sync.dma_start(
+                out=k_scales[32 * quad : 32 * quad + 4, :].bitcast(I32),
+                in_=keys_scales[0, 4 * quad : 4 * quad + 4, :].bitcast(I32),
+            )
+        k_words_hbm = keys_words[0].rearrange("p t r -> p (t r)").bitcast(I32)
+        k_words = []
+        for b in range(T // BANK):
+            tile = keep.tile([P, BANK], I32, name="k_words%d" % b, align_bytes=64)
+            nc.sync.dma_start(out=tile[:], in_=k_words_hbm[:, b * BANK : (b + 1) * BANK])
+            k_words.append(tile)
+        drop_list = keep.tile([P, I // 16], U16, name="drop_list")
+        gain_list = keep.tile([P, I // 16], U16, name="gain_list")
+        share_col = keep.tile([P, PACK], F32, name="share_col")
+        nc.gpsimd.dma_start(out=share_col[:], in_=share.rearrange("o (p j) -> p (o j)", j=PACK))
+        v_raw = {}
+        for g in range(PASSES):
+            rows = vals[g * K_PASS : (g + 1) * K_PASS, :].rearrange("(p j) e -> p j e", j=PACK)
+            for h in range(2):
+                tile = keep.tile([P, PACK, E_HALF], F32, name="v_raw%d%d" % (g, h))
+                nc.sync.dma_start(out=tile[:], in_=rows[:, :, h * E_HALF : (h + 1) * E_HALF])
+                v_raw[g, h] = tile
+                if (g, h) == (0, 0):
+                    nc.sync.dma_start(drop_list[:], offs)
+                if (g, h) == (0, 1):
+                    nc.sync.dma_start(gain_list[:], offs2)
+
+        ident = keep.tile([P, P], F32, name="ident")
+        make_identity(nc, ident[:])
+        fac_col = keep.tile([P, PASSES, PACK], F32, name="fac_col")
+        nc.gpsimd.dma_start(out=fac_col[:], in_=fac.rearrange("o (g p j) -> p (o g) j", g=PASSES, j=PACK))
+        minus_one = keep.tile([P, I_HALF], F32, name="minus_one")
+        nc.vector.memset(minus_one[:], -1.0)
+        warm = keep.tile([P, 1], F32, name="warm")
+        nc.scalar.activation(warm[:], minus_one[:, 0:1], ACT.Exp)
+        taken = keep.tile([P, T], F32, name="taken")
+        nc.vector.memset(taken[:], 0.0)
+        given = keep.tile([P, T], F32, name="given")
+        nc.vector.memset(given[:], 0.0)
+
+        q_grouped = keep.tile([P, Q, PACK], BF16, name="q_grouped", align_bytes=64)
+        dst, src = interleave_views(q_grouped[:], q_raw[:])
+        nc.vector.tensor_copy(out=dst, in_=src)
+        q_codes = keep.tile([P, Q], U32, name="q_codes", align_bytes=64)
+        q_scales = keep.tile([P, Q], U8, name="q_scales", align_bytes=64)
+        nc.vector.quantize_mx(
+            out=q_codes[:].bitcast(FP8X4), scales=q_scales[:], in_=q_grouped[:].rearrange("p q j -> p (q j)")
+        )
+
+        scores = keep.tile([P, T], F32, name="scores")
+        row_max = None
+        for b in range(T // BANK):
+            cols = slice(b * BANK, (b + 1) * BANK)
+            bank = psum.tile([P, BANK], F32, name="score_bank%d" % b)
+            nc.tensor.matmul_mx(
+                out=bank[:],
+                lhsT=q_codes[:].bitcast(FP8X4),
+                lhsT_scale=q_scales[:],
+                rhs=k_words[b][:].bitcast(FP8X4),
+                rhs_scale=k_scales[:, cols],
+                start=True,
+                stop=True,
+            )
+            running_max = keep.tile([P, 1], F32, name="running_max%d" % b)
+            nc.vector.tensor_scalar(
+                out=scores[:, cols], in0=bank[:], scalar1=1.0, scalar2=row_max,
+                op0=ALU.mult, op1=ALU.max, accum_out=running_max[:],
+            )
+            row_max = running_max[:]
+        neg_max = keep.tile([P, 1], F32, name="neg_max")
+        nc.scalar.activation(neg_max[:], row_max, ACT.Copy, scale=-1.0)
+        picked = []
+        for s in range(2):
+            tile = keep.tile([P, I_HALF], F32, name="picked%d" % s, tag="picked%d" % s, align_bytes=64)
+            entries = drop_list[:, s * I_HALF // 16 : (s + 1) * I_HALF // 16]
+            nc.vector.tensor_copy(tile[:], scores[:].indirect(entries))
+            picked.append(tile)
+
+        share_bank = psum.tile([P, PACK, P], F32, name="share_bank")
+        for j in range(PACK):
+            nc.tensor.transpose(share_bank[:, j, :], share_col[:, j : j + 1].to_broadcast([P, P]), ident[:])
+        share_rows = keep.tile([P, I], F32, name="share_rows", tag="share_rows", align_bytes=64)
+        nc.scalar.copy(
+            out=share_rows[:].rearrange("m (n j) -> m n j", j=PACK), in_=share_bank[:].rearrange("m j n -> m n j")
+        )
+
+        r = keep.tile([P, I], F32, name="r")
+        p_all = keep.tile([P, T], F32, name="p_all")
+        part_sums = [keep.tile([P, 1], F32, name="part_sum%d" % s) for s in range(2)]
+        nc.scalar.activation(
+            p_all[:, :P_FIRST], scores[:, :P_FIRST], ACT.Exp, bias=neg_max[:], accum_out=part_sums[0][:]
+        )
+        row_sum = keep.tile([P, 1], F32, name="row_sum")
+        inv_sum = keep.tile([P, 1], F32, name="inv_sum")
+        for s in range(2):
+            slots = slice(s * I_HALF, (s + 1) * I_HALF)
+            entries = drop_list[:, s * I_HALF // 16 : (s + 1) * I_HALF // 16]
+            nc.scalar.activation(r[:, slots], picked[s][:], ACT.Exp, bias=neg_max[:])
+            nc.vector.tensor_tensor(taken[:].indirect(entries), r[:, slots], minus_one[:], ALU.mult)
+            if s == 0:
+                nc.scalar.activation(
+                    p_all[:, P_FIRST:], scores[:, P_FIRST:], ACT.Exp, bias=neg_max[:], accum_out=part_sums[1][:]
+                )
+                nc.scalar.activation(row_sum[:], part_sums[0][:], ACT.Identity, bias=part_sums[1][:])
+                nc.vector.reciprocal(inv_sum[:], row_sum[:])
+        nc.vector.tensor_tensor(given[:].indirect(gain_list[:]), r[:], share_rows[:], ALU.mult)
+
+        inv_bank = psum.tile([P, P], F32, name="inv_bank")
+        nc.tensor.transpose(inv_bank[:], inv_sum[:].to_broadcast([P, P]), ident[:])
+        factor = []
+        for g in range(PASSES):
+            tile = keep.tile([P, PACK, Q], F32, name="factor%d" % g)
+            for j in range(PACK):
+                nc.scalar.activation(tile[:, j, :], inv_bank[:], ACT.Copy, scale=fac_col[:, g, j : j + 1])
+            factor.append(tile)
+
+        v_codes = keep.tile([P, PASSES * E], U32, name="v_codes", align_bytes=64)
+        v_scales = keep.tile([P, PASSES * E], U8, name="v_scales", tag="share_rows", align_bytes=64)
+        v_early = keep.tile([P, E_EARLY * PACK], BF16, name="v_early", align_bytes=64)
+        v_late = keep.tile([P, (PASSES * E - E_EARLY) * PACK], BF16, name="v_late", tag="picked1", align_bytes=64)
+
+        def grouped(lo, hi):
+            if hi <= E_EARLY:
+                return v_early[:, lo * PACK : hi * PACK]
+            return v_late[:, (lo - E_EARLY) * PACK : (hi - E_EARLY) * PACK]
+
+        for lo, hi in ((0, E_EARLY), (E_EARLY, E_HALF), (E_HALF, E), (E, E + E_HALF), (E + E_HALF, 2 * E)):
+            piece = lo // E_HALF
+            raw = v_raw[piece // 2, piece % 2][:, :, lo - piece * E_HALF : hi - piece * E_HALF]
+            dst, src = interleave_views(grouped(lo, hi).rearrange("p (e j) -> p e j", j=PACK), raw)
+            nc.scalar.copy(out=dst, in_=src)
+        for lo, hi in ((0, E_EARLY), (E_EARLY, E_HALF), (E_HALF, E), (E, 2 * E)):
+            nc.vector.quantize_mx(out=v_codes[:, lo:hi].bitcast(FP8X4), scales=v_scales[:, lo:hi], in_=grouped(lo, hi))
+
+        w_banks = [psum.tile([P, PACK, Q], F32, name="w_bank%d" % g) for g in range(PASSES)]
+        terms = (p_all, taken, given)
+        for n, term in enumerate(terms):
+            for g in range(PASSES):
+                for j in range(PACK):
+                    nc.tensor.matmul(
+                        w_banks[g][:, j, :],
+                        lhsT=term[:, g * K_PASS + j : (g + 1) * K_PASS : PACK],
+                        rhs=ident[:],
+                        is_transpose=True,
+                        start=(n == 0 and j == 0),
+                        stop=(n == len(terms) - 1 and j == PACK - 1),
+                    )
+
+        out_banks = [psum.tile([P, E_HALF], F32, name="out_bank%d" % h) for h in range(2)]
+        for g in range(PASSES):
+            w_grouped = keep.tile([P, Q, PACK], BF16, name="w_grouped%d" % g, align_bytes=64)
+            nc.vector.tensor_tensor(
+                out=w_grouped[:],
+                in0=w_banks[g][:].rearrange("p j q -> p q j"),
+                in1=factor[g][:].rearrange("p j q -> p q j"),
+                op=ALU.mult,
+            )
+            w_codes = keep.tile([P, Q], U32, name="w_codes%d" % g, align_bytes=64)
+            w_scales = keep.tile([P, Q], U8, name="w_scales%d" % g, align_bytes=64)
+            nc.vector.quantize_mx(
+                out=w_codes[:].bitcast(FP8X4), scales=w_scales[:], in_=w_grouped[:].rearrange("p q j -> p (q j)")
+            )
+            for h in range(2):
+                v_cols = slice(g * E + h * E_HALF, g * E + (h + 1) * E_HALF)
+                nc.tensor.matmul_mx(
+                    out=out_banks[h][:],
+                    lhsT=w_codes[:].bitcast(FP8X4),
+                    lhsT_scale=w_scales[:],
+                    rhs=v_codes[:, v_cols].bitcast(FP8X4),
+                    rhs_scale=v_scales[:, v_cols],
+                    start=(g == 0),
+                    stop=(g == PASSES - 1),
+                )
+
+        for h in range(2):
+            result = keep.tile([P, E_HALF], F32, name="result%d" % h)
+            cols = slice(h * E_HALF, (h + 1) * E_HALF)
+            if h == 0:
+                nc.scalar.copy(out=result[:], in_=out_banks[h][:])
+                nc.scalar.dma_start(out=out[:, cols], in_=result[:])
+            else:
+                nc.vector.tensor_copy(out=result[:], in_=out_banks[h][:])
+                nc.sync.dma_start(out=out[:, cols], in_=result[:])

@@ -59,7 +59,7 @@ def tile_attend_passedon_heads_kernel(tc, query, keys_words, keys_scales, share,
         drop_list = keep.tile([P, I // 16], U16, name="drop_list")
         gain_list = keep.tile([P, I // 16], U16, name="gain_list")
         share_col = keep.tile([P, PACK], F32, name="share_col")
-        nc.gpsimd.dma_start(out=share_col[:], in_=share.rearrange("o (p j) -> p (o j)", j=PACK))
+        nc.scalar.dma_start(out=share_col[:], in_=share.rearrange("o (p j) -> p (o j)", j=PACK))
         v_raw = {}
         for g in range(PASSES):
             rows = vals[g * K_PASS : (g + 1) * K_PASS, :].rearrange("(p j) e -> p j e", j=PACK)
@@ -72,10 +72,11 @@ def tile_attend_passedon_heads_kernel(tc, query, keys_words, keys_scales, share,
                 if (g, h) == (0, 1):
                     nc.sync.dma_start(gain_list[:], offs2)
 
+        fac_col = keep.tile([P, PASSES, PACK], F32, name="fac_col")
+        nc.sync.dma_start(out=fac_col[:], in_=fac.rearrange("o (g p j) -> p (o g) j", g=PASSES, j=PACK))
+
         ident = keep.tile([P, P], F32, name="ident")
         make_identity(nc, ident[:])
-        fac_col = keep.tile([P, PASSES, PACK], F32, name="fac_col")
-        nc.gpsimd.dma_start(out=fac_col[:], in_=fac.rearrange("o (g p j) -> p (o g) j", g=PASSES, j=PACK))
         minus_one = keep.tile([P, I_HALF], F32, name="minus_one")
         nc.vector.memset(minus_one[:], -1.0)
         warm = keep.tile([P, 1], F32, name="warm")
@@ -152,15 +153,6 @@ def tile_attend_passedon_heads_kernel(tc, query, keys_words, keys_scales, share,
                 nc.vector.reciprocal(inv_sum[:], row_sum[:])
         nc.vector.tensor_tensor(given[:].indirect(gain_list[:]), r[:], share_rows[:], ALU.mult)
 
-        inv_bank = psum.tile([P, P], F32, name="inv_bank")
-        nc.tensor.transpose(inv_bank[:], inv_sum[:].to_broadcast([P, P]), ident[:])
-        factor = []
-        for g in range(PASSES):
-            tile = keep.tile([P, PACK, Q], F32, name="factor%d" % g)
-            for j in range(PACK):
-                nc.scalar.activation(tile[:, j, :], inv_bank[:], ACT.Copy, scale=fac_col[:, g, j : j + 1])
-            factor.append(tile)
-
         v_codes = keep.tile([P, PASSES * E], U32, name="v_codes", align_bytes=64)
         v_scales = keep.tile([P, PASSES * E], U8, name="v_scales", tag="share_rows", align_bytes=64)
         v_early = keep.tile([P, E_EARLY * PACK], BF16, name="v_early", align_bytes=64)
@@ -178,6 +170,15 @@ def tile_attend_passedon_heads_kernel(tc, query, keys_words, keys_scales, share,
             nc.scalar.copy(out=dst, in_=src)
         for lo, hi in ((0, E_EARLY), (E_EARLY, E_HALF), (E_HALF, E), (E, 2 * E)):
             nc.vector.quantize_mx(out=v_codes[:, lo:hi].bitcast(FP8X4), scales=v_scales[:, lo:hi], in_=grouped(lo, hi))
+
+        inv_bank = psum.tile([P, P], F32, name="inv_bank")
+        nc.tensor.transpose(inv_bank[:], inv_sum[:].to_broadcast([P, P]), ident[:])
+        factor = []
+        for g in range(PASSES):
+            tile = keep.tile([P, PACK, Q], F32, name="factor%d" % g)
+            for j in range(PACK):
+                nc.scalar.activation(tile[:, j, :], inv_bank[:], ACT.Copy, scale=fac_col[:, g, j : j + 1])
+            factor.append(tile)
 
         w_banks = [psum.tile([P, PACK, Q], F32, name="w_bank%d" % g) for g in range(PASSES)]
         terms = (p_all, taken, given)
@@ -197,9 +198,9 @@ def tile_attend_passedon_heads_kernel(tc, query, keys_words, keys_scales, share,
         for g in range(PASSES):
             w_grouped = keep.tile([P, Q, PACK], BF16, name="w_grouped%d" % g, align_bytes=64)
             nc.vector.tensor_tensor(
-                out=w_grouped[:],
-                in0=w_banks[g][:].rearrange("p j q -> p q j"),
-                in1=factor[g][:].rearrange("p j q -> p q j"),
+                out=w_grouped[:].rearrange("p (c i) j -> p c j i", i=LINE),
+                in0=w_banks[g][:].rearrange("p j (c i) -> p c j i", i=LINE),
+                in1=factor[g][:].rearrange("p j (c i) -> p c j i", i=LINE),
                 op=ALU.mult,
             )
             w_codes = keep.tile([P, Q], U32, name="w_codes%d" % g, align_bytes=64)

@@ -24,7 +24,8 @@ BANK = 512
 E_HALF = E // 2
 I_HALF = I // 2
 LINE = 4
-P_FIRST = 384
+Q_VECTOR = 72
+SCORE_PIECES = ((0, 256), (256, 512), (512, 1024))
 E_EARLY = 128
 
 
@@ -45,33 +46,31 @@ def tile_attend_passedon_heads_kernel(tc, query, keys_words, keys_scales, share,
         nc.vector.memset(k_scales[:].bitcast(I32), 0)
         q_raw = keep.tile([P, PACK, Q], F32, name="q_raw")
         nc.sync.dma_start(out=q_raw[:], in_=query.rearrange("(p j) q -> p j q", j=PACK))
-        for quad in range(4):
-            nc.sync.dma_start(
-                out=k_scales[32 * quad : 32 * quad + 4, :].bitcast(I32),
-                in_=keys_scales[0, 4 * quad : 4 * quad + 4, :].bitcast(I32),
-            )
         k_words_hbm = keys_words[0].rearrange("p t r -> p (t r)").bitcast(I32)
         k_words = []
         for b in range(T // BANK):
             tile = keep.tile([P, BANK], I32, name="k_words%d" % b, align_bytes=64)
             nc.sync.dma_start(out=tile[:], in_=k_words_hbm[:, b * BANK : (b + 1) * BANK])
             k_words.append(tile)
+            if b == 0:
+                for quad in range(4):
+                    nc.sync.dma_start(
+                        out=k_scales[32 * quad : 32 * quad + 4, :].bitcast(I32),
+                        in_=keys_scales[0, 4 * quad : 4 * quad + 4, :].bitcast(I32),
+                    )
         drop_list = keep.tile([P, I // 16], U16, name="drop_list")
         gain_list = keep.tile([P, I // 16], U16, name="gain_list")
+        nc.sync.dma_start(drop_list[:], offs)
+        v_rows = vals.rearrange("(g p j) e -> g p j e", p=P, j=PACK)
+        v_raw_early = keep.tile([P, PACK, E_EARLY], F32, name="v_raw_early")
+        nc.sync.dma_start(out=v_raw_early[:], in_=v_rows[0][:, :, :E_EARLY])
         share_col = keep.tile([P, PACK], F32, name="share_col")
-        nc.scalar.dma_start(out=share_col[:], in_=share.rearrange("o (p j) -> p (o j)", j=PACK))
-        v_raw = {}
-        for g in range(PASSES):
-            rows = vals[g * K_PASS : (g + 1) * K_PASS, :].rearrange("(p j) e -> p j e", j=PACK)
-            for h in range(2):
-                tile = keep.tile([P, PACK, E_HALF], F32, name="v_raw%d%d" % (g, h))
-                nc.sync.dma_start(out=tile[:], in_=rows[:, :, h * E_HALF : (h + 1) * E_HALF])
-                v_raw[g, h] = tile
-                if (g, h) == (0, 0):
-                    nc.sync.dma_start(drop_list[:], offs)
-                if (g, h) == (0, 1):
-                    nc.sync.dma_start(gain_list[:], offs2)
-
+        nc.sync.dma_start(out=share_col[:], in_=share.rearrange("o (p j) -> p (o j)", j=PACK))
+        v_raw_rest = keep.tile([P, PACK, E - E_EARLY], F32, name="v_raw_rest")
+        nc.sync.dma_start(out=v_raw_rest[:], in_=v_rows[0][:, :, E_EARLY:])
+        nc.sync.dma_start(gain_list[:], offs2)
+        v_raw_last = keep.tile([P, PACK, E], F32, name="v_raw_last")
+        nc.sync.dma_start(out=v_raw_last[:], in_=v_rows[1])
         fac_col = keep.tile([P, PASSES, PACK], F32, name="fac_col")
         nc.sync.dma_start(out=fac_col[:], in_=fac.rearrange("o (g p j) -> p (o g) j", g=PASSES, j=PACK))
 
@@ -87,8 +86,10 @@ def tile_attend_passedon_heads_kernel(tc, query, keys_words, keys_scales, share,
         nc.vector.memset(given[:], 0.0)
 
         q_grouped = keep.tile([P, Q, PACK], BF16, name="q_grouped", align_bytes=64)
-        dst, src = interleave_views(q_grouped[:], q_raw[:])
+        dst, src = interleave_views(q_grouped[:, :Q_VECTOR, :], q_raw[:, :, :Q_VECTOR])
         nc.vector.tensor_copy(out=dst, in_=src)
+        dst, src = interleave_views(q_grouped[:, Q_VECTOR:, :], q_raw[:, :, Q_VECTOR:])
+        nc.scalar.copy(out=dst, in_=src)
         q_codes = keep.tile([P, Q], U32, name="q_codes", align_bytes=64)
         q_scales = keep.tile([P, Q], U8, name="q_scales", align_bytes=64)
         nc.vector.quantize_mx(
@@ -96,48 +97,35 @@ def tile_attend_passedon_heads_kernel(tc, query, keys_words, keys_scales, share,
         )
 
         scores = keep.tile([P, T], F32, name="scores")
-        row_max = None
-        for b in range(T // BANK):
-            cols = slice(b * BANK, (b + 1) * BANK)
-            bank = psum.tile([P, BANK], F32, name="score_bank%d" % b)
+        piece_max = keep.tile([P, len(SCORE_PIECES)], F32, name="piece_max")
+        for n, (lo, hi) in enumerate(SCORE_PIECES):
+            cols = slice(lo, hi)
+            bank = psum.tile([P, hi - lo], F32, name="score_bank%d" % n)
             nc.tensor.matmul_mx(
                 out=bank[:],
                 lhsT=q_codes[:].bitcast(FP8X4),
                 lhsT_scale=q_scales[:],
-                rhs=k_words[b][:].bitcast(FP8X4),
+                rhs=k_words[lo // BANK][:, lo % BANK : lo % BANK + hi - lo].bitcast(FP8X4),
                 rhs_scale=k_scales[:, cols],
                 start=True,
                 stop=True,
             )
-            running_max = keep.tile([P, 1], F32, name="running_max%d" % b)
             nc.vector.tensor_scalar(
-                out=scores[:, cols], in0=bank[:], scalar1=1.0, scalar2=row_max,
-                op0=ALU.mult, op1=ALU.max, accum_out=running_max[:],
+                out=scores[:, cols], in0=bank[:], scalar1=1.0, scalar2=None,
+                op0=ALU.mult, op1=ALU.max, accum_out=piece_max[:, n : n + 1],
             )
-            row_max = running_max[:]
         neg_max = keep.tile([P, 1], F32, name="neg_max")
-        nc.scalar.activation(neg_max[:], row_max, ACT.Copy, scale=-1.0)
         picked = []
         for s in range(2):
             tile = keep.tile([P, I_HALF], F32, name="picked%d" % s, tag="picked%d" % s, align_bytes=64)
             entries = drop_list[:, s * I_HALF // 16 : (s + 1) * I_HALF // 16]
             nc.vector.tensor_copy(tile[:], scores[:].indirect(entries))
             picked.append(tile)
-
-        share_bank = psum.tile([P, PACK, P], F32, name="share_bank")
-        for j in range(PACK):
-            nc.tensor.transpose(share_bank[:, j, :], share_col[:, j : j + 1].to_broadcast([P, P]), ident[:])
-        share_rows = keep.tile([P, I], F32, name="share_rows", tag="share_rows", align_bytes=64)
-        nc.scalar.copy(
-            out=share_rows[:].rearrange("m (n j) -> m n j", j=PACK), in_=share_bank[:].rearrange("m j n -> m n j")
-        )
+            if s == 0:
+                nc.vector.tensor_reduce(neg_max[:], piece_max[:], mybir.AxisListType.X, ALU.max, negate=True)
 
         r = keep.tile([P, I], F32, name="r")
         p_all = keep.tile([P, T], F32, name="p_all")
-        part_sums = [keep.tile([P, 1], F32, name="part_sum%d" % s) for s in range(2)]
-        nc.scalar.activation(
-            p_all[:, :P_FIRST], scores[:, :P_FIRST], ACT.Exp, bias=neg_max[:], accum_out=part_sums[0][:]
-        )
         row_sum = keep.tile([P, 1], F32, name="row_sum")
         inv_sum = keep.tile([P, 1], F32, name="inv_sum")
         for s in range(2):
@@ -146,17 +134,22 @@ def tile_attend_passedon_heads_kernel(tc, query, keys_words, keys_scales, share,
             nc.scalar.activation(r[:, slots], picked[s][:], ACT.Exp, bias=neg_max[:])
             nc.vector.tensor_tensor(taken[:].indirect(entries), r[:, slots], minus_one[:], ALU.mult)
             if s == 0:
-                nc.scalar.activation(
-                    p_all[:, P_FIRST:], scores[:, P_FIRST:], ACT.Exp, bias=neg_max[:], accum_out=part_sums[1][:]
-                )
-                nc.scalar.activation(row_sum[:], part_sums[0][:], ACT.Identity, bias=part_sums[1][:])
+                nc.scalar.activation(p_all[:], scores[:], ACT.Exp, bias=neg_max[:], accum_out=row_sum[:])
                 nc.vector.reciprocal(inv_sum[:], row_sum[:])
+        share_bank = psum.tile([P, PACK, P], F32, name="share_bank", tag="spread_bank")
+        for j in range(PACK):
+            nc.tensor.transpose(share_bank[:, j, :], share_col[:, j : j + 1].to_broadcast([P, P]), ident[:])
+        share_rows = keep.tile([P, I], F32, name="share_rows", tag="picked1", align_bytes=64)
+        nc.scalar.copy(
+            out=share_rows[:].rearrange("m (n j) -> m n j", j=PACK), in_=share_bank[:].rearrange("m j n -> m n j")
+        )
+
         nc.vector.tensor_tensor(given[:].indirect(gain_list[:]), r[:], share_rows[:], ALU.mult)
 
         v_codes = keep.tile([P, PASSES * E], U32, name="v_codes", align_bytes=64)
-        v_scales = keep.tile([P, PASSES * E], U8, name="v_scales", tag="share_rows", align_bytes=64)
+        v_scales = keep.tile([P, PASSES * E], U8, name="v_scales", tag="picked1", align_bytes=64)
         v_early = keep.tile([P, E_EARLY * PACK], BF16, name="v_early", align_bytes=64)
-        v_late = keep.tile([P, (PASSES * E - E_EARLY) * PACK], BF16, name="v_late", tag="picked1", align_bytes=64)
+        v_late = keep.tile([P, (PASSES * E - E_EARLY) * PACK], BF16, name="v_late", tag="picked0", align_bytes=64)
 
         def grouped(lo, hi):
             if hi <= E_EARLY:
@@ -164,14 +157,18 @@ def tile_attend_passedon_heads_kernel(tc, query, keys_words, keys_scales, share,
             return v_late[:, (lo - E_EARLY) * PACK : (hi - E_EARLY) * PACK]
 
         for lo, hi in ((0, E_EARLY), (E_EARLY, E_HALF), (E_HALF, E), (E, E + E_HALF), (E + E_HALF, 2 * E)):
-            piece = lo // E_HALF
-            raw = v_raw[piece // 2, piece % 2][:, :, lo - piece * E_HALF : hi - piece * E_HALF]
+            if hi <= E_EARLY:
+                raw = v_raw_early[:, :, lo:hi]
+            elif hi <= E:
+                raw = v_raw_rest[:, :, lo - E_EARLY : hi - E_EARLY]
+            else:
+                raw = v_raw_last[:, :, lo - E : hi - E]
             dst, src = interleave_views(grouped(lo, hi).rearrange("p (e j) -> p e j", j=PACK), raw)
             nc.scalar.copy(out=dst, in_=src)
         for lo, hi in ((0, E_EARLY), (E_EARLY, E_HALF), (E_HALF, E), (E, 2 * E)):
             nc.vector.quantize_mx(out=v_codes[:, lo:hi].bitcast(FP8X4), scales=v_scales[:, lo:hi], in_=grouped(lo, hi))
 
-        inv_bank = psum.tile([P, P], F32, name="inv_bank")
+        inv_bank = psum.tile([P, P], F32, name="inv_bank", tag="spread_bank")
         nc.tensor.transpose(inv_bank[:], inv_sum[:].to_broadcast([P, P]), ident[:])
         factor = []
         for g in range(PASSES):

from contextlib import ExitStack

import concourse.mybir as mybir
from concourse.masks import make_identity

D, T, Q, I, E = 512, 1024, 128, 512, 512
FLOPS = 2 * Q * D * T + 2 * Q * T * E

F32 = mybir.dt.float32
BF16 = mybir.dt.bfloat16
I32 = mybir.dt.int32
U32 = mybir.dt.uint32
U16 = mybir.dt.uint16
U8 = mybir.dt.uint8
FP8X4 = mybir.dt.float8_e4m3fn_x4
ALU = mybir.AluOpType
ACT = mybir.ActivationFunctionType

P = 128
PACK = 4
K_PASS = P * PACK
PASSES = T // K_PASS
BANK = 512
E_HALF = E // 2
I_HALF = I // 2
LINE = 4
Q_VECTOR = 72
SCORE_PIECES = ((0, 256), (256, 512), (512, 1024))
E_EARLY = 128


def interleave_views(dst, src):
    return (
        dst.rearrange("p (c i) j -> p c j i", i=LINE),
        src.rearrange("p j (c i) -> p c j i", i=LINE),
    )


def tile_attend_passedon_heads_kernel(tc, query, keys_words, keys_scales, share, fac, vals, offs, offs2, out):
    nc = tc.nc
    with ExitStack() as ctx:
        keep = ctx.enter_context(tc.tile_pool(name="keep", bufs=1))
        psum = ctx.enter_context(tc.psum_pool(name="psum", bufs=1))

        k_scales = keep.tile([P, T], U8, name="k_scales", align_bytes=64)
        nc.vector.memset(k_scales[:].bitcast(I32), 0)
        q_raw = keep.tile([P, PACK, Q], F32, name="q_raw")
        nc.sync.dma_start(out=q_raw[:], in_=query.rearrange("(p j) q -> p j q", j=PACK))
        k_words_hbm = keys_words[0].rearrange("p t r -> p (t r)").bitcast(I32)
        k_words = []
        for b in range(T // BANK):
            tile = keep.tile([P, BANK], I32, name="k_words%d" % b, align_bytes=64)
            nc.sync.dma_start(out=tile[:], in_=k_words_hbm[:, b * BANK : (b + 1) * BANK])
            k_words.append(tile)
            if b == 0:
                for quad in range(4):
                    nc.sync.dma_start(
                        out=k_scales[32 * quad : 32 * quad + 4, :].bitcast(I32),
                        in_=keys_scales[0, 4 * quad : 4 * quad + 4, :].bitcast(I32),
                    )
        drop_list = keep.tile([P, I // 16], U16, name="drop_list")
        gain_list = keep.tile([P, I // 16], U16, name="gain_list")
        nc.sync.dma_start(drop_list[:], offs)
        v_rows = vals.rearrange("(g p j) e -> g p j e", p=P, j=PACK)
        v_raw_early = keep.tile([P, PACK, E_EARLY], F32, name="v_raw_early")
        nc.sync.dma_start(out=v_raw_early[:], in_=v_rows[0][:, :, :E_EARLY])
        share_col = keep.tile([P, PACK], F32, name="share_col")
        nc.sync.dma_start(out=share_col[:], in_=share.rearrange("o (p j) -> p (o j)", j=PACK))
        v_raw_rest = keep.tile([P, PACK, E - E_EARLY], F32, name="v_raw_rest")
        nc.sync.dma_start(out=v_raw_rest[:], in_=v_rows[0][:, :, E_EARLY:])
        nc.sync.dma_start(gain_list[:], offs2)
        v_raw_last = keep.tile([P, PACK, E], F32, name="v_raw_last")
        nc.sync.dma_start(out=v_raw_last[:], in_=v_rows[1])
        fac_col = keep.tile([P, PASSES, PACK], F32, name="fac_col")
        nc.sync.dma_start(out=fac_col[:], in_=fac.rearrange("o (g p j) -> p (o g) j", g=PASSES, j=PACK))

        ident = keep.tile([P, P], F32, name="ident")
        make_identity(nc, ident[:])
        minus_one = keep.tile([P, I_HALF], F32, name="minus_one")
        nc.vector.memset(minus_one[:], -1.0)
        warm = keep.tile([P, 1], F32, name="warm")
        nc.scalar.activation(warm[:], minus_one[:, 0:1], ACT.Exp)
        taken = keep.tile([P, T], F32, name="taken")
        nc.vector.memset(taken[:], 0.0)
        given = keep.tile([P, T], F32, name="given")
        nc.vector.memset(given[:], 0.0)

        q_grouped = keep.tile([P, Q, PACK], BF16, name="q_grouped", align_bytes=64)
        dst, src = interleave_views(q_grouped[:, :Q_VECTOR, :], q_raw[:, :, :Q_VECTOR])
        nc.vector.tensor_copy(out=dst, in_=src)
        dst, src = interleave_views(q_grouped[:, Q_VECTOR:, :], q_raw[:, :, Q_VECTOR:])
        nc.scalar.copy(out=dst, in_=src)
        q_codes = keep.tile([P, Q], U32, name="q_codes", align_bytes=64)
        q_scales = keep.tile([P, Q], U8, name="q_scales", align_bytes=64)
        nc.vector.quantize_mx(
            out=q_codes[:].bitcast(FP8X4), scales=q_scales[:], in_=q_grouped[:].rearrange("p q j -> p (q j)")
        )

        scores = keep.tile([P, T], F32, name="scores")
        piece_max = keep.tile([P, len(SCORE_PIECES)], F32, name="piece_max")
        for n, (lo, hi) in enumerate(SCORE_PIECES):
            cols = slice(lo, hi)
            bank = psum.tile([P, hi - lo], F32, name="score_bank%d" % n)
            nc.tensor.matmul_mx(
                out=bank[:],
                lhsT=q_codes[:].bitcast(FP8X4),
                lhsT_scale=q_scales[:],
                rhs=k_words[lo // BANK][:, lo % BANK : lo % BANK + hi - lo].bitcast(FP8X4),
                rhs_scale=k_scales[:, cols],
                start=True,
                stop=True,
            )
            nc.vector.tensor_scalar(
                out=scores[:, cols], in0=bank[:], scalar1=1.0, scalar2=None,
                op0=ALU.mult, op1=ALU.max, accum_out=piece_max[:, n : n + 1],
            )
        neg_max = keep.tile([P, 1], F32, name="neg_max")
        picked = []
        for s in range(2):
            tile = keep.tile([P, I_HALF], F32, name="picked%d" % s, tag="picked%d" % s, align_bytes=64)
            entries = drop_list[:, s * I_HALF // 16 : (s + 1) * I_HALF // 16]
            nc.vector.tensor_copy(tile[:], scores[:].indirect(entries))
            picked.append(tile)
            if s == 0:
                nc.vector.tensor_reduce(neg_max[:], piece_max[:], mybir.AxisListType.X, ALU.max, negate=True)

        r = keep.tile([P, I], F32, name="r")
        p_all = keep.tile([P, T], F32, name="p_all")
        row_sum = keep.tile([P, 1], F32, name="row_sum")
        inv_sum = keep.tile([P, 1], F32, name="inv_sum")
        for s in range(2):
            slots = slice(s * I_HALF, (s + 1) * I_HALF)
            entries = drop_list[:, s * I_HALF // 16 : (s + 1) * I_HALF // 16]
            nc.scalar.activation(r[:, slots], picked[s][:], ACT.Exp, bias=neg_max[:])
            nc.vector.tensor_tensor(taken[:].indirect(entries), r[:, slots], minus_one[:], ALU.mult)
            if s == 0:
                nc.scalar.activation(p_all[:], scores[:], ACT.Exp, bias=neg_max[:], accum_out=row_sum[:])
                nc.vector.reciprocal(inv_sum[:], row_sum[:])
        share_bank = psum.tile([P, PACK, P], F32, name="share_bank", tag="spread_bank")
        for j in range(PACK):
            nc.tensor.transpose(share_bank[:, j, :], share_col[:, j : j + 1].to_broadcast([P, P]), ident[:])
        share_rows = keep.tile([P, I], F32, name="share_rows", tag="picked1", align_bytes=64)
        nc.scalar.copy(
            out=share_rows[:].rearrange("m (n j) -> m n j", j=PACK), in_=share_bank[:].rearrange("m j n -> m n j")
        )

        nc.vector.tensor_tensor(given[:].indirect(gain_list[:]), r[:], share_rows[:], ALU.mult)

        v_codes = keep.tile([P, PASSES * E], U32, name="v_codes", align_bytes=64)
        v_scales = keep.tile([P, PASSES * E], U8, name="v_scales", tag="picked1", align_bytes=64)
        v_early = keep.tile([P, E_EARLY * PACK], BF16, name="v_early", align_bytes=64)
        v_late = keep.tile([P, (PASSES * E - E_EARLY) * PACK], BF16, name="v_late", tag="picked0", align_bytes=64)

        def grouped(lo, hi):
            if hi <= E_EARLY:
                return v_early[:, lo * PACK : hi * PACK]
            return v_late[:, (lo - E_EARLY) * PACK : (hi - E_EARLY) * PACK]

        for lo, hi in ((0, E_EARLY), (E_EARLY, E_HALF), (E_HALF, E), (E, E + E_HALF), (E + E_HALF, 2 * E)):
            if hi <= E_EARLY:
                raw = v_raw_early[:, :, lo:hi]
            elif hi <= E:
                raw = v_raw_rest[:, :, lo - E_EARLY : hi - E_EARLY]
            else:
                raw = v_raw_last[:, :, lo - E : hi - E]
            dst, src = interleave_views(grouped(lo, hi).rearrange("p (e j) -> p e j", j=PACK), raw)
            nc.scalar.copy(out=dst, in_=src)
        for lo, hi in ((0, E_EARLY), (E_EARLY, E_HALF), (E_HALF, E), (E, 2 * E)):
            nc.vector.quantize_mx(out=v_codes[:, lo:hi].bitcast(FP8X4), scales=v_scales[:, lo:hi], in_=grouped(lo, hi))

        inv_bank = psum.tile([P, P], F32, name="inv_bank", tag="spread_bank")
        nc.tensor.transpose(inv_bank[:], inv_sum[:].to_broadcast([P, P]), ident[:])
        factor = []
        for g in range(PASSES):
            tile = keep.tile([P, PACK, Q], F32, name="factor%d" % g)
            for j in range(PACK):
                nc.scalar.activation(tile[:, j, :], inv_bank[:], ACT.Copy, scale=fac_col[:, g, j : j + 1])
            factor.append(tile)

        w_banks = [psum.tile([P, PACK, Q], F32, name="w_bank%d" % g) for g in range(PASSES)]
        terms = (p_all, taken, given)
        for n, term in enumerate(terms):
            for g in range(PASSES):
                for j in range(PACK):
                    nc.tensor.matmul(
                        w_banks[g][:, j, :],
                        lhsT=term[:, g * K_PASS + j : (g + 1) * K_PASS : PACK],
                        rhs=ident[:],
                        is_transpose=True,
                        start=(n == 0 and j == 0),
                        stop=(n == len(terms) - 1 and j == PACK - 1),
                    )

        out_banks = [psum.tile([P, E_HALF], F32, name="out_bank%d" % h) for h in range(2)]
        for g in range(PASSES):
            w_grouped = keep.tile([P, Q, PACK], BF16, name="w_grouped%d" % g, align_bytes=64)
            nc.vector.tensor_tensor(
                out=w_grouped[:].rearrange("p (c i) j -> p c j i", i=LINE),
                in0=w_banks[g][:].rearrange("p j (c i) -> p c j i", i=LINE),
                in1=factor[g][:].rearrange("p j (c i) -> p c j i", i=LINE),
                op=ALU.mult,
            )
            w_codes = keep.tile([P, Q], U32, name="w_codes%d" % g, align_bytes=64)
            w_scales = keep.tile([P, Q], U8, name="w_scales%d" % g, align_bytes=64)
            nc.vector.quantize_mx(
                out=w_codes[:].bitcast(FP8X4), scales=w_scales[:], in_=w_grouped[:].rearrange("p q j -> p (q j)")
            )
            for h in range(2):
                v_cols = slice(g * E + h * E_HALF, g * E + (h + 1) * E_HALF)
                nc.tensor.matmul_mx(
                    out=out_banks[h][:],
                    lhsT=w_codes[:].bitcast(FP8X4),
                    lhsT_scale=w_scales[:],
                    rhs=v_codes[:, v_cols].bitcast(FP8X4),
                    rhs_scale=v_scales[:, v_cols],
                    start=(g == 0),
                    stop=(g == PASSES - 1),
                )

        for h in range(2):
            result = keep.tile([P, E_HALF], F32, name="result%d" % h)
            cols = slice(h * E_HALF, (h + 1) * E_HALF)
            if h == 0:
                nc.scalar.copy(out=result[:], in_=out_banks[h][:])
                nc.scalar.dma_start(out=out[:, cols], in_=result[:])
            else:
                nc.vector.tensor_copy(out=result[:], in_=out_banks[h][:])
                nc.sync.dma_start(out=out[:, cols], in_=result[:])
